import numpy as np
import ml_dtypes


def mxq(x, axis, fmt="e4m3"):
    dtype, down = {"e4m3": (ml_dtypes.float8_e4m3fn, 7), "e5m2": (ml_dtypes.float8_e5m2, 14)}[fmt]
    v = np.moveaxis(np.asarray(x, np.float32).astype(ml_dtypes.bfloat16).astype(np.float64), axis, -1)
    blocks = v.reshape(v.shape[:-1] + (-1, 32))
    amax = np.abs(blocks).max(-1, keepdims=True)
    byte = np.maximum(np.where(amax > 0, np.frexp(amax)[1] - 1 + 127, 0) - down, 1)
    scale = np.exp2(byte - 127.0)
    codes = (blocks / scale).astype(np.float32).astype(dtype).astype(np.float64)
    return np.moveaxis((codes * scale).reshape(v.shape), -1, axis)


WIDE = False


def mx_kscale(k):
    if not WIDE:
        return np.ones(k)
    levels = np.array([30, -30])
    if k % 512:
        return np.exp2(np.random.permutation(np.resize(levels, k // 32))).repeat(32)
    a = np.empty((k // 512, 16))
    for p in range(k // 512):
        a[p, :8] = np.random.permutation(np.resize(levels, 8))
        for g in range(8):
            far = levels[np.abs(levels - a[p, g]) >= 10]
            a[p, g + 8] = far[np.random.randint(len(far))]
    return np.exp2(a.ravel()).repeat(32)


def f64(x):
    return np.asarray(x).astype(np.float64)


def striped(idx):
    return np.tile(idx.reshape(-1, 16).T, (8, 1)).astype(np.uint16)


def unstriped(offs):
    return offs[:16].T.reshape(-1).astype(np.int64)


E2M1 = np.array([0.0, 0.5, 1.0, 1.5, 2.0, 3.0, 4.0, 6.0, -0.0, -0.5, -1.0, -1.5, -2.0, -3.0, -4.0, -6.0])


def pack_weight(w, fmt):
    k, n = w.shape
    w = f64(np.asarray(w, np.float32).astype(ml_dtypes.bfloat16)).reshape(k // 32, 32, n)
    amax = np.abs(w).max(1)
    if fmt == "e4m3":
        byte = np.frexp(amax)[1] - 1 + 127 - 7
    elif fmt == "e5m2":
        byte = np.frexp(amax)[1] - 1 + 127 - 14
    else:
        mant, ex = np.frexp(amax / 6.0)
        byte = np.where(mant > 0.5, ex, ex - 1) + 127
    byte = np.clip(np.where(amax > 0, byte, 1), 1, 254)
    scaled = (w * np.exp2(127.0 - byte)[:, None, :]).reshape(k, n).astype(np.float32)
    by_word = np.ascontiguousarray(scaled.reshape(k // 512, 128, 4, n).transpose(0, 1, 3, 2))
    if fmt == "e4m3":
        words = by_word.astype(ml_dtypes.float8_e4m3fn).view(np.uint8)
    elif fmt == "e5m2":
        words = by_word.astype(ml_dtypes.float8_e5m2).view(np.uint8)
    else:
        c = by_word.astype(ml_dtypes.float4_e2m1fn).view(np.uint8) & 0xF
        words = (c[..., 0::2] | (c[..., 1::2] << 4)).reshape(k // 512, 128, 2 * n)
    return np.ascontiguousarray(words), np.ascontiguousarray(byte.astype(np.uint8).reshape(k // 512, 16, n))


def unpack_weight(words, scales, fmt):
    g, _, n = scales.shape
    words = np.ascontiguousarray(words).reshape(g, 128, n, -1)
    if fmt == "e4m3":
        vals = words.view(ml_dtypes.float8_e4m3fn).astype(np.float64)
    elif fmt == "e5m2":
        vals = words.view(ml_dtypes.float8_e5m2).astype(np.float64)
    else:
        nib = np.empty((g, 128, n, 4), np.uint8)
        nib[..., 0::2] = words & 0xF
        nib[..., 1::2] = words >> 4
        vals = E2M1[nib]
    vals = vals * np.repeat(np.exp2(scales.astype(np.float64) - 127.0), 8, axis=1)[..., None]
    return vals.transpose(0, 1, 3, 2).reshape(g * 512, n)


K, T, E, C, N = 128, 1024, 8, 512, 1024
TOP = 4


def by_expert(wq, xq):
    return np.concatenate([wq[e].T @ xq[:, e * C:(e + 1) * C] for e in range(E)], axis=1)


def setup_inputs():
    n = np.random.standard_normal
    s = mx_kscale(N)[:, None]
    deal = np.repeat(np.arange(E), C).reshape(TOP, T)[:, np.random.permutation(T)]
    deal = np.take_along_axis(deal, np.argsort(np.random.rand(TOP, T), axis=0), axis=0)
    for _ in range(8):
        s_, t_ = np.random.permutation(T).reshape(2, -1); r = np.random.randint(TOP, size=T // 2); x, y = deal[r, s_].copy(), deal[r, t_].copy()
        ok = ~((deal[:, s_] == y).any(0) | (deal[:, t_] == x).any(0)); deal[r[ok], s_[ok]] = y[ok]; deal[r[ok], t_[ok]] = x[ok]
    order = np.lexsort((np.random.rand(TOP * T), deal.reshape(-1)))
    slot_token = order % T; pos = np.empty(TOP * T, np.int64); pos[order] = np.arange(TOP * T); pos = pos.reshape(TOP, T)
    g = np.random.uniform(0.5, 1.5, (TOP, T)); g = g / g.sum(0)
    w_slot = np.empty(E * C)
    for r in range(TOP): w_slot[pos[r]] = g[r]
    dy = pack_weight(n((N, T)) * s, "e5m2")
    return {
        "dy_words": dy[0],
        "dy_scales": dy[1],
        "w": (n((E + 1, N, K)) / np.sqrt(N) / s[None]).astype(np.float32),
        "gate": np.tile(w_slot, (K, 1)).astype(np.float32),
        "offs": striped(slot_token),
        "pos1": striped(pos[0]),
        "pos2": striped(pos[1]),
        "pos3": striped(pos[2]),
        "pos4": striped(pos[3]),
    }


def reference(dy_words, dy_scales, w, gate, offs, pos1, pos2, pos3, pos4):
    idx = unstriped(offs)
    gq = unpack_weight(dy_words, dy_scales, "e5m2")[:, idx]
    wq = mxq(f64(w), 1, "e4m3")
    ds = wq[E].T @ unpack_weight(dy_words, dy_scales, "e5m2")
    dx = f64(gate) * by_expert(wq, gq)
    return ds + dx[:, unstriped(pos1)] + dx[:, unstriped(pos2)] + dx[:, unstriped(pos3)] + dx[:, unstriped(pos4)]

@@ -1,0 +1,145 @@
+from contextlib import ExitStack
+
+import concourse.mybir as mybir
+
+F32 = mybir.dt.float32
+BF16 = mybir.dt.bfloat16
+I32 = mybir.dt.int32
+U32 = mybir.dt.uint32
+U16 = mybir.dt.uint16
+U8 = mybir.dt.uint8
+E4M3 = mybir.dt.float8_e4m3fn_x4
+E5M2 = mybir.dt.float8_e5m2_x4
+MULT = mybir.AluOpType.mult
+ADD = mybir.AluOpType.add
+
+P = 128
+K, T, E, C, N = 128, 1024, 8, 512, 1024
+S = E * C
+PASSES = 2
+PAIR = 2 * C
+SPARE = 352
+FLOPS = 2 * K * N * (S + T)
+
+
+def tile_moe_bds_lin_none_kernel(tc, dy_words, dy_scales, w, gate, offs, pos1, pos2, pos3, pos4, out):
+    nc = tc.nc
+    with ExitStack() as ctx:
+        lists = ctx.enter_context(tc.tile_pool(name="lists", bufs=1))
+        keep = ctx.enter_context(tc.tile_pool(name="keep", bufs=1))
+        psum = ctx.enter_context(tc.psum_pool(name="psum", bufs=1))
+
+        slot_token = lists.tile([P, S // 16], U16, name="slot_token")
+        nc.sync.dma_start(slot_token[:], offs)
+
+        words = keep.tile([P, PASSES * T + SPARE], I32, name="words", align_bytes=64)
+        planes = keep.tile([P, 4 * T], U8, name="planes", align_bytes=64)
+        plane1 = keep.tile([P, T], U8, name="plane1", align_bytes=64)
+        nc.vector.memset(planes[:, 0:T].bitcast(I32), 0)
+        for o in range(PASSES):
+            nc.sync.dma_start(words[:, o * T:(o + 1) * T], dy_words[o].rearrange("p t d -> p (t d)").bitcast(I32))
+        for q in range(4):
+            nc.scalar.dma_start(planes[32 * q:32 * q + 8, 0:T].bitcast(I32), dy_scales[:, 4 * q:4 * q + 4, :].bitcast(I32))
+        nc.vector.memset(words[:, PASSES * T:], 0)
+        nc.vector.memset(planes[:, T:].bitcast(I32), 0)
+        nc.vector.memset(plane1[:].bitcast(I32), 0)
+        slot_plane0 = [keep.tile([P, S // 2], U8, name=f"slot_plane0_{h}", align_bytes=64) for h in range(2)]
+        slot_plane1 = [keep.tile([P, S // 2], U8, name=f"slot_plane1_{h}", align_bytes=64) for h in range(2)]
+        for h in range(2):
+            nc.vector.memset(slot_plane1[h][:].bitcast(I32), 0)
+
+        def load_w(e0, n, tag):
+            raw = keep.tile([P, n * PASSES, 4, K], F32, name="raw", tag=tag)
+            nc.sync.dma_start(raw[:].rearrange("p g j k -> p g (j k)"),
+                              w[e0:e0 + n].rearrange("e (o p j) k -> p (e o) (j k)", o=PASSES, j=4))
+            return raw
+
+        def round_w(raw, n, tag):
+            rounded = keep.tile([P, n * PASSES, K, 4], BF16, name="rounded", tag=tag, align_bytes=64)
+            nc.scalar.copy(rounded[:].rearrange("p g (c i) j -> p g c j i", i=4),
+                           raw[:].rearrange("p g j (c i) -> p g c j i", i=4))
+            return rounded
+
+        def quantize_w(rounded, n, name):
+            codes = keep.tile([P, n * PASSES * K], U32, name=name + "_codes", align_bytes=64)
+            scales = keep.tile([P, n * PASSES * K], U8, name=name + "_scales", align_bytes=64)
+            nc.vector.quantize_mx(out=codes[:].bitcast(E4M3), scales=scales[:], in_=rounded[:].rearrange("p g k j -> p (g k j)"))
+            return codes, scales
+
+        def product(bank, codes, scales, first, moving, moving_scales):
+            for o in range(PASSES):
+                cols = slice((first + o) * K, (first + o + 1) * K)
+                nc.tensor.matmul_mx(out=bank[:], lhsT=codes[:, cols].bitcast(E4M3), lhsT_scale=scales[:, cols],
+                                    rhs=moving[o].bitcast(E5M2), rhs_scale=moving_scales[o],
+                                    start=(o == 0), stop=(o == PASSES - 1))
+
+        raw_shared = load_w(E, 1, "raw_shared")
+        raws = [load_w(2 * c, 2, f"raw{c}") for c in range(E // 2)]
+        slot_lists = []
+        for r, pos in enumerate((pos1, pos2, pos3, pos4)):
+            t = lists.tile([P, T // 16], U16, name=f"slot_list{r}")
+            nc.sync.dma_start(t[:], pos)
+            slot_lists.append(t)
+
+        windows = [words[:, 0:2 * T].bitcast(U32), words[:, T:].bitcast(U32)]
+
+        def gather_words(c, tag, piece):
+            got = keep.tile([P, PASSES * PAIR], U32, name="got", tag=tag, align_bytes=64)
+            for a in range(0, PAIR, piece):
+                for o in range(PASSES):
+                    cols = slice((c * PAIR + a) // 16, (c * PAIR + a + piece) // 16)
+                    nc.vector.tensor_copy(got[:, o * PAIR + a:o * PAIR + a + piece], windows[o].indirect(slot_token[:, cols]))
+            return got
+
+        got = {0: gather_words(0, "got0", PAIR)}
+        for h in range(2):
+            cols = slice(h * (S // 32), (h + 1) * (S // 32))
+            nc.vector.tensor_copy(slot_plane0[h][:], planes[:].indirect(slot_token[:, cols]))
+            nc.sync.dma_start(slot_plane1[h][0:100, :].bitcast(I32), slot_plane0[h][4:104, :].bitcast(I32))
+        nc.sync.dma_start(plane1[0:100, :].bitcast(I32), planes[4:104, 0:T].bitcast(I32))
+
+        codes, scales = quantize_w(round_w(raw_shared, 1, "rounded_shared"), 1, "shared")
+        ds = keep.tile([P, T], F32, name="ds")
+        for h in range(2):
+            cols = slice(h * C, (h + 1) * C)
+            bank = psum.tile([P, C], F32, name="shared_bank", bufs=2)
+            product(bank, codes, scales, 0,
+                    [words[:, o * T + h * C:o * T + (h + 1) * C] for o in range(PASSES)],
+                    [planes[:, cols], plane1[:, cols]])
+            nc.scalar.copy(ds[:, cols], bank[:])
+
+        dx = keep.tile([P, S], F32, name="dx")
+        banks = {}
+
+        def apply_gate(c, tag):
+            g = keep.tile([P, PAIR], F32, name="g", tag=tag)
+            nc.sync.dma_start(g[:], gate[:, c * PAIR:(c + 1) * PAIR])
+            for i in range(2):
+                e = 2 * c + i
+                nc.vector.tensor_tensor(dx[:, e * C:(e + 1) * C], banks[e][:], g[:, i * C:(i + 1) * C], MULT)
+
+        for c in range(E // 2):
+            rounded = round_w(raws[c], 2, f"stage{c}")
+            codes, scales = quantize_w(rounded, 2, f"pair{c}")
+            if c > 0:
+                got[c] = gather_words(c, f"stage{c}", PAIR if c < E // 2 - 1 else C)
+            for i in range(2):
+                e = 2 * c + i
+                banks[e] = psum.tile([P, C], F32, name="bank", bufs=6)
+                h, a = divmod(e * C, S // 2)
+                product(banks[e], codes, scales, 2 * i,
+                        [got[c][:, o * PAIR + i * C:o * PAIR + (i + 1) * C] for o in range(PASSES)],
+                        [slot_plane0[h][:, a:a + C], slot_plane1[h][:, a:a + C]])
+            if c > 0:
+                apply_gate(c - 1, f"raw{c}")
+        apply_gate(E // 2 - 1, "raw_shared")
+
+        sums = [ds[:, 0:C], ds[:, C:T]]
+        for r in range(4):
+            for h in range(2):
+                total = keep.tile([P, C], F32, name=f"total{r}_{h}")
+                cols = slice(h * (C // 16), (h + 1) * (C // 16))
+                nc.vector.tensor_tensor(total[:], dx[:].indirect(slot_lists[r][:, cols]), sums[h], ADD)
+                sums[h] = total[:]
+        for h in range(2):
+            nc.sync.dma_start(out[:, h * C:(h + 1) * C], sums[h])

@@ -1,6 +1,7 @@
 from contextlib import ExitStack
 
 import concourse.mybir as mybir
+from concourse.masks import make_identity
 
 F32 = mybir.dt.float32
 BF16 = mybir.dt.bfloat16
@@ -12,6 +13,7 @@ E4M3 = mybir.dt.float8_e4m3fn_x4
 E5M2 = mybir.dt.float8_e5m2_x4
 MULT = mybir.AluOpType.mult
 ADD = mybir.AluOpType.add
+COPY = mybir.ActivationFunctionType.Copy
 
 P = 128
 K, T, E, C, N = 128, 1024, 8, 512, 1024
@@ -19,6 +21,7 @@ S = E * C
 PASSES = 2
 PAIR = 2 * C
 SPARE = 352
+TURNED = 4
 FLOPS = 2 * K * N * (S + T)
 
 
@@ -32,36 +35,44 @@ def tile_moe_bds_lin_none_kernel(tc, dy_words, dy_scales, w, gate, offs, pos1, p
         slot_token = lists.tile([P, S // 16], U16, name="slot_token")
         nc.sync.dma_start(slot_token[:], offs)
 
-        words = keep.tile([P, PASSES * T + SPARE], I32, name="words", align_bytes=64)
-        planes = keep.tile([P, 4 * T], U8, name="planes", align_bytes=64)
-        plane1 = keep.tile([P, T], U8, name="plane1", align_bytes=64)
-        nc.vector.memset(planes[:, 0:T].bitcast(I32), 0)
-        for o in range(PASSES):
-            nc.sync.dma_start(words[:, o * T:(o + 1) * T], dy_words[o].rearrange("p t d -> p (t d)").bitcast(I32))
+        words = [keep.tile([P, T + SPARE], I32, name=f"words{o}", align_bytes=64) for o in range(PASSES)]
+        planes = keep.tile([P, T + SPARE], U8, name="planes", align_bytes=64)
         for q in range(4):
-            nc.scalar.dma_start(planes[32 * q:32 * q + 8, 0:T].bitcast(I32), dy_scales[:, 4 * q:4 * q + 4, :].bitcast(I32))
-        nc.vector.memset(words[:, PASSES * T:], 0)
+            nc.sync.dma_start(planes[32 * q + 24:32 * q + 32, 0:T].bitcast(I32), dy_scales[:, 4 * q:4 * q + 4, :].bitcast(I32))
+            nc.vector.memset(planes[32 * q:32 * q + 24, 0:T].bitcast(I32), 0)
         nc.vector.memset(planes[:, T:].bitcast(I32), 0)
-        nc.vector.memset(plane1[:].bitcast(I32), 0)
-        slot_plane0 = [keep.tile([P, S // 2], U8, name=f"slot_plane0_{h}", align_bytes=64) for h in range(2)]
-        slot_plane1 = [keep.tile([P, S // 2], U8, name=f"slot_plane1_{h}", align_bytes=64) for h in range(2)]
-        for h in range(2):
-            nc.vector.memset(slot_plane1[h][:].bitcast(I32), 0)
+        for o in range(PASSES):
+            nc.gpsimd.memset(words[o][:, T:], 0)
+        identity = keep.tile([P, P], F32, name="identity")
+        make_identity(nc, identity[:])
+        gate_rows = keep.tile([P, P], F32, name="gate_rows")
+        nc.gpsimd.memset(gate_rows[:], 0.0)
+        turned_blocks = TURNED * C // P
 
-        def load_w(e0, n, tag):
-            raw = keep.tile([P, n * PASSES, 4, K], F32, name="raw", tag=tag)
-            nc.sync.dma_start(raw[:].rearrange("p g j k -> p g (j k)"),
-                              w[e0:e0 + n].rearrange("e (o p j) k -> p (e o) (j k)", o=PASSES, j=4))
+        live_planes = [keep.tile([P, S // 2], U8, name=f"live_plane{o}", align_bytes=64) for o in range(PASSES)]
+        for plane in live_planes:
+            nc.gpsimd.memset(plane[96:128, :].bitcast(I32), 0)
+
+        def spread(source, width):
+            for o in range(PASSES):
+                nc.sync.dma_start(live_planes[o][0:100, 0:width].bitcast(I32), source[24 + 4 * o:124 + 4 * o, 0:width].bitcast(I32))
+
+        def load_w(e):
+            raw = keep.tile([P, PASSES, 4, K], F32, name="raw", tag=f"raw{e}", align_bytes=64)
+            nc.sync.dma_start(raw[:].rearrange("p g j k -> p g (j k)"), w[e].rearrange("(o p j) k -> p o (j k)", o=PASSES, j=4))
             return raw
 
-        def round_w(raw, n, tag):
-            rounded = keep.tile([P, n * PASSES, K, 4], BF16, name="rounded", tag=tag, align_bytes=64)
-            nc.scalar.copy(rounded[:].rearrange("p g (c i) j -> p g c j i", i=4),
-                           raw[:].rearrange("p g j (c i) -> p g c j i", i=4))
+        def load_words(o):
+            nc.sync.dma_start(words[o][:, 0:T], dy_words[o].rearrange("p t d -> p (t d)").bitcast(I32))
+
+        def round_w(sources, tag):
+            rounded = keep.tile([P, len(sources) * PASSES, K, 4], BF16, name="rounded", tag=tag, align_bytes=64)
+            for i, raw in enumerate(sources):
+                nc.scalar.copy(rounded[:, i * PASSES:(i + 1) * PASSES], raw[:].rearrange("p g j k -> p g k j"))
             return rounded
 
-        def quantize_w(rounded, n, name):
-            codes = keep.tile([P, n * PASSES * K], U32, name=name + "_codes", align_bytes=64)
+        def quantize_w(rounded, n, name, tag):
+            codes = keep.tile([P, n * PASSES * K], U32, name="codes", tag=tag, align_bytes=64)
             scales = keep.tile([P, n * PASSES * K], U8, name=name + "_scales", align_bytes=64)
             nc.vector.quantize_mx(out=codes[:].bitcast(E4M3), scales=scales[:], in_=rounded[:].rearrange("p g k j -> p (g k j)"))
             return codes, scales
@@ -73,15 +84,30 @@ def tile_moe_bds_lin_none_kernel(tc, dy_words, dy_scales, w, gate, offs, pos1, p
                                     rhs=moving[o].bitcast(E5M2), rhs_scale=moving_scales[o],
                                     start=(o == 0), stop=(o == PASSES - 1))
 
-        raw_shared = load_w(E, 1, "raw_shared")
-        raws = [load_w(2 * c, 2, f"raw{c}") for c in range(E // 2)]
+        def gather_bytes(h, tag):
+            packed = keep.tile([P, S // 2], U8, name="packed", tag=tag, align_bytes=64)
+            for i in range(2):
+                a = (2 * h + i) * (PAIR // 16)
+                nc.vector.tensor_copy(packed[:, i * PAIR:(i + 1) * PAIR], planes[:].indirect(slot_token[:, a:a + PAIR // 16]))
+            return packed
+
+        packed = [gather_bytes(h, f"packed{h}") for h in range(2)]
+        raws = [load_w(e) for e in range(4)]
+        for o in range(PASSES):
+            load_words(o)
+        raws.extend(load_w(e) for e in range(4, 6))
+        spread(packed[0], S // 2)
+        nc.sync.dma_start(gate_rows[0:turned_blocks, :], gate[0, 0:TURNED * C].rearrange("(b m) -> b m", m=P))
+        raws.extend(load_w(e) for e in range(6, E + 1))
+        gate_tail = keep.tile([P, S - TURNED * C], F32, name="gate_tail")
+        nc.sync.dma_start(gate_tail[:], gate[:, TURNED * C:])
         slot_lists = []
         for r, pos in enumerate((pos1, pos2, pos3, pos4)):
             t = lists.tile([P, T // 16], U16, name=f"slot_list{r}")
             nc.sync.dma_start(t[:], pos)
             slot_lists.append(t)
 
-        windows = [words[:, 0:2 * T].bitcast(U32), words[:, T:].bitcast(U32)]
+        windows = [words[o][:].bitcast(U32) for o in range(PASSES)]
 
         def gather_words(c, tag, piece):
             got = keep.tile([P, PASSES * PAIR], U32, name="got", tag=tag, align_bytes=64)
@@ -92,54 +118,104 @@ def tile_moe_bds_lin_none_kernel(tc, dy_words, dy_scales, w, gate, offs, pos1, p
             return got
 
         got = {0: gather_words(0, "got0", PAIR)}
-        for h in range(2):
-            cols = slice(h * (S // 32), (h + 1) * (S // 32))
-            nc.vector.tensor_copy(slot_plane0[h][:], planes[:].indirect(slot_token[:, cols]))
-            nc.sync.dma_start(slot_plane1[h][0:100, :].bitcast(I32), slot_plane0[h][4:104, :].bitcast(I32))
-        nc.sync.dma_start(plane1[0:100, :].bitcast(I32), planes[4:104, 0:T].bitcast(I32))
+        roundeds = [round_w(raws[2 * c:2 * c + 2], f"stage{c}") for c in range(E // 2)]
+        gate_bank = psum.tile([P, P], F32, name="gate_bank", tag="G")
+        nc.tensor.transpose(gate_bank[:], gate_rows[:], identity[:])
+        gate_cols = keep.tile([P, turned_blocks], F32, name="gate_cols", tag="raw5", align_bytes=64)
+        nc.scalar.copy(gate_cols[:], gate_bank[:, 0:turned_blocks])
 
-        codes, scales = quantize_w(round_w(raw_shared, 1, "rounded_shared"), 1, "shared")
-        ds = keep.tile([P, T], F32, name="ds")
-        for h in range(2):
-            cols = slice(h * C, (h + 1) * C)
-            bank = psum.tile([P, C], F32, name="shared_bank", bufs=2)
-            product(bank, codes, scales, 0,
-                    [words[:, o * T + h * C:o * T + (h + 1) * C] for o in range(PASSES)],
-                    [planes[:, cols], plane1[:, cols]])
-            nc.scalar.copy(ds[:, cols], bank[:])
 
         dx = keep.tile([P, S], F32, name="dx")
         banks = {}
+        product_tag = "ACBDACGE"
+        turned_tag = "BDAC"
+        back_tag = "EFEF"
 
-        def apply_gate(c, tag):
-            g = keep.tile([P, PAIR], F32, name="g", tag=tag)
-            nc.sync.dma_start(g[:], gate[:, c * PAIR:(c + 1) * PAIR])
-            for i in range(2):
-                e = 2 * c + i
-                nc.vector.tensor_tensor(dx[:, e * C:(e + 1) * C], banks[e][:], g[:, i * C:(i + 1) * C], MULT)
+        def turn(bank, source):
+            for b in range(C // P):
+                nc.tensor.transpose(bank[:, b * P:(b + 1) * P], source[:, b * P:(b + 1) * P], identity[:])
+
+        def gate_turned(e, plain):
+            nc.scalar.copy(plain, banks[e][:])
+            turned = psum.tile([P, C], F32, name="turned", tag=turned_tag[e])
+            turn(turned, plain)
+            gated = keep.tile([P, C], F32, name="gated", bufs=3)
+            for b in range(C // P):
+                col = e * (C // P) + b
+                nc.scalar.activation(gated[:, b * P:(b + 1) * P], turned[:, b * P:(b + 1) * P], COPY, scale=gate_cols[:, col:col + 1])
+            back = psum.tile([P, C], F32, name="back", tag=back_tag[e])
+            turn(back, gated)
+            nc.scalar.copy(dx[:, e * C:(e + 1) * C], back[:])
 
         for c in range(E // 2):
-            rounded = round_w(raws[c], 2, f"stage{c}")
-            codes, scales = quantize_w(rounded, 2, f"pair{c}")
+            codes, scales = quantize_w(roundeds[c], 2, f"pair{c}", f"codes{c}")
             if c > 0:
-                got[c] = gather_words(c, f"stage{c}", PAIR if c < E // 2 - 1 else C)
+                got[c] = gather_words(c, f"stage{c}", PAIR if c < 2 else C)
+            if 2 * c < TURNED:
+                plain = keep.tile([P, PAIR], F32, name="plain", tag=f"raw{E - 1 - c}", align_bytes=64)
+            if c == 2:
+                spread(packed[1], S // 2)
+            if c == 3:
+                spread(planes, T)
             for i in range(2):
                 e = 2 * c + i
-                banks[e] = psum.tile([P, C], F32, name="bank", bufs=6)
-                h, a = divmod(e * C, S // 2)
+                banks[e] = psum.tile([P, C], F32, name="bank", tag=product_tag[e])
+                a = e * C % (S // 2)
                 product(banks[e], codes, scales, 2 * i,
                         [got[c][:, o * PAIR + i * C:o * PAIR + (i + 1) * C] for o in range(PASSES)],
-                        [slot_plane0[h][:, a:a + C], slot_plane1[h][:, a:a + C]])
-            if c > 0:
-                apply_gate(c - 1, f"raw{c}")
-        apply_gate(E // 2 - 1, "raw_shared")
+                        [plane[:, a:a + C] for plane in live_planes])
+                if e < TURNED:
+                    gate_turned(e, plain[:, i * C:(i + 1) * C])
 
-        sums = [ds[:, 0:C], ds[:, C:T]]
-        for r in range(4):
-            for h in range(2):
-                total = keep.tile([P, C], F32, name=f"total{r}_{h}")
-                cols = slice(h * (C // 16), (h + 1) * (C // 16))
-                nc.vector.tensor_tensor(total[:], dx[:].indirect(slot_lists[r][:, cols]), sums[h], ADD)
-                sums[h] = total[:]
-        for h in range(2):
-            nc.sync.dma_start(out[:, h * C:(h + 1) * C], sums[h])
+        codes, scales = quantize_w(round_w(raws[E:], "raw6"), 1, "shared", "codes2")
+        for e in range(TURNED, E):
+            nc.vector.tensor_tensor(dx[:, e * C:(e + 1) * C], banks[e][:], gate_tail[:, (e - TURNED) * C:(e - TURNED + 1) * C], MULT)
+
+        ds = [None, None]
+        for h, tag in ((1, "A"), (0, "C")):
+            cols = slice(h * C, (h + 1) * C)
+            bank = psum.tile([P, C], F32, name="shared_bank", tag=tag)
+            product(bank, codes, scales, 0,
+                    [words[o][:, cols] for o in range(PASSES)],
+                    [plane[:, cols] for plane in live_planes])
+            ds[h] = keep.tile([P, C], F32, name=f"ds{h}")
+            nc.scalar.copy(ds[h][:], bank[:])
+
+        def add_on_tensor(h, count, tags):
+            terms = [ds[h]]
+            for r in range(count):
+                fetched = keep.tile([P, C], F32, name=f"fetched{h}_{r}")
+                nc.vector.tensor_copy(fetched[:], dx[:].indirect(slot_lists[r][:, h * (C // 16):(h + 1) * (C // 16)]))
+                terms.append(fetched)
+            width = C // len(tags)
+            turned = [psum.tile([P, width], F32, name="turned_sum", tag=pair[0]) for pair in tags]
+            for n, term in enumerate(terms):
+                for b in range(C // P):
+                    i, a = divmod(b * P, width)
+                    nc.tensor.matmul(turned[i][:, a:a + P], term[:, b * P:(b + 1) * P], identity[:], is_transpose=True,
+                                     start=(n == 0 and a == 0), stop=(n == count and a + P == width))
+            totals = []
+            for i, pair in enumerate(tags):
+                held = keep.tile([P, width], F32, name=f"held{h}_{i}")
+                nc.scalar.copy(held[:], turned[i][:])
+                back = psum.tile([P, width], F32, name="back_sum", tag=pair[1])
+                for a in range(0, width, P):
+                    nc.tensor.transpose(back[:, a:a + P], held[:, a:a + P], identity[:])
+                total = keep.tile([P, width], F32, name=f"total{h}_{i}")
+                nc.scalar.copy(total[:], back[:])
+                totals.append(total)
+            return totals
+
+        partial = add_on_tensor(1, 2, ["GH"])[0]
+        for i, total in enumerate(add_on_tensor(0, 4, ["BE", "DF"])):
+            nc.scalar.dma_start(out[:, i * (C // 2):(i + 1) * (C // 2)], total[:])
+        quarter = C // 2
+        sums = [partial[:, 0:quarter], partial[:, quarter:C]]
+        for r in (2, 3):
+            for i in range(2):
+                total = keep.tile([P, quarter], F32, name=f"last{r}_{i}")
+                a = (C + i * quarter) // 16
+                nc.vector.tensor_tensor(total[:], dx[:].indirect(slot_lists[r][:, a:a + quarter // 16]), sums[i], ADD)
+                sums[i] = total[:]
+        for i in range(2):
+            nc.sync.dma_start(out[:, C + i * quarter:C + (i + 1) * quarter], sums[i])

@@ -19,10 +19,21 @@ P = 128
 K, T, E, C, N = 128, 1024, 8, 512, 1024
 S = E * C
 PASSES = 2
+PACK = 4
+QUADRANT = 32
+PER_COLUMN = 16
 PAIR = 2 * C
+BLOCKS = C // P
 SPARE = 352
+STAGED_ROW = QUADRANT - PASSES * PACK
+PLANE_ROWS = 3 * QUADRANT + PACK
+PLANE_COLUMNS = 3 * PAIR
 TURNED = 4
 FLOPS = 2 * K * N * (S + T)
+
+PRODUCT_BANK = "ACBDACEF"
+TURNED_BANK = "BDAC"
+BACK_BANK = "EFEF"
 
 
 def tile_moe_bds_lin_none_kernel(tc, dy_words, dy_scales, w, gate, offs, pos1, pos2, pos3, pos4, out):
@@ -32,190 +43,193 @@ def tile_moe_bds_lin_none_kernel(tc, dy_words, dy_scales, w, gate, offs, pos1, p
         keep = ctx.enter_context(tc.tile_pool(name="keep", bufs=1))
         psum = ctx.enter_context(tc.psum_pool(name="psum", bufs=1))
 
-        slot_token = lists.tile([P, S // 16], U16, name="slot_token")
+        slot_token = lists.tile([P, S // PER_COLUMN], U16, name="slot_token")
         nc.sync.dma_start(slot_token[:], offs)
 
-        words = [keep.tile([P, T + SPARE], I32, name=f"words{o}", align_bytes=64) for o in range(PASSES)]
-        planes = keep.tile([P, T + SPARE], U8, name="planes", align_bytes=64)
-        for q in range(4):
-            nc.sync.dma_start(planes[32 * q + 24:32 * q + 32, 0:T].bitcast(I32), dy_scales[:, 4 * q:4 * q + 4, :].bitcast(I32))
-            nc.vector.memset(planes[32 * q:32 * q + 24, 0:T].bitcast(I32), 0)
-        nc.vector.memset(planes[:, T:].bitcast(I32), 0)
-        for o in range(PASSES):
-            nc.gpsimd.memset(words[o][:, T:], 0)
+        words = keep.tile([P, PASSES * T + SPARE], I32, name="words", align_bytes=64)
+        token_scales = keep.tile([P, T + SPARE], U8, name="token_scales", align_bytes=64)
+        for q in range(P // QUADRANT):
+            row = QUADRANT * q
+            nc.sync.dma_start(token_scales[row + STAGED_ROW:row + QUADRANT, 0:T].bitcast(I32),
+                              dy_scales[:, PACK * q:PACK * (q + 1), :].bitcast(I32))
+            nc.vector.memset(token_scales[row:row + STAGED_ROW, 0:T].bitcast(I32), 0)
+        nc.vector.memset(token_scales[:, T:].bitcast(I32), 0)
+        nc.vector.memset(words[:, PASSES * T:], 0)
         identity = keep.tile([P, P], F32, name="identity")
         make_identity(nc, identity[:])
         gate_rows = keep.tile([P, P], F32, name="gate_rows")
         nc.gpsimd.memset(gate_rows[:], 0.0)
-        turned_blocks = TURNED * C // P
+        turned_blocks = TURNED * BLOCKS
 
-        live_planes = [keep.tile([P, S // 2], U8, name=f"live_plane{o}", align_bytes=64) for o in range(PASSES)]
-        for plane in live_planes:
-            nc.gpsimd.memset(plane[96:128, :].bitcast(I32), 0)
+        planes = [keep.tile([P, PLANE_COLUMNS], U8, name=f"plane{o}", align_bytes=64) for o in range(PASSES)]
+        for plane in planes:
+            nc.vector.memset(plane[:].bitcast(I32), 0)
 
-        def spread(source, width):
+        def fill_planes(staged, first):
+            width = staged.shape[1]
             for o in range(PASSES):
-                nc.sync.dma_start(live_planes[o][0:100, 0:width].bitcast(I32), source[24 + 4 * o:124 + 4 * o, 0:width].bitcast(I32))
+                row = STAGED_ROW + PACK * o
+                nc.sync.dma_start(planes[o][0:PLANE_ROWS, first:first + width].bitcast(I32),
+                                  staged[row:row + PLANE_ROWS, :].bitcast(I32))
 
         def load_w(e):
-            raw = keep.tile([P, PASSES, 4, K], F32, name="raw", tag=f"raw{e}", align_bytes=64)
-            nc.sync.dma_start(raw[:].rearrange("p g j k -> p g (j k)"), w[e].rearrange("(o p j) k -> p o (j k)", o=PASSES, j=4))
+            raw = keep.tile([P, PASSES, PACK, K], F32, name="raw", tag=f"raw{e}", align_bytes=64)
+            nc.sync.dma_start(raw[:].rearrange("p o j k -> p o (j k)"),
+                              w[e].rearrange("(o p j) k -> p o (j k)", o=PASSES, j=PACK))
             return raw
 
-        def load_words(o):
-            nc.sync.dma_start(words[o][:, 0:T], dy_words[o].rearrange("p t d -> p (t d)").bitcast(I32))
-
         def round_w(sources, tag):
-            rounded = keep.tile([P, len(sources) * PASSES, K, 4], BF16, name="rounded", tag=tag, align_bytes=64)
+            rounded = keep.tile([P, len(sources) * PASSES, K, PACK], BF16, name="rounded", tag=tag, align_bytes=64)
             for i, raw in enumerate(sources):
-                nc.scalar.copy(rounded[:, i * PASSES:(i + 1) * PASSES], raw[:].rearrange("p g j k -> p g k j"))
+                nc.scalar.copy(rounded[:, i * PASSES:(i + 1) * PASSES], raw[:].rearrange("p o j k -> p o k j"))
             return rounded
 
-        def quantize_w(rounded, n, name, tag):
-            codes = keep.tile([P, n * PASSES * K], U32, name="codes", tag=tag, align_bytes=64)
-            scales = keep.tile([P, n * PASSES * K], U8, name=name + "_scales", align_bytes=64)
-            nc.vector.quantize_mx(out=codes[:].bitcast(E4M3), scales=scales[:], in_=rounded[:].rearrange("p g k j -> p (g k j)"))
+        def quantize_w(rounded, name, tag):
+            width = rounded.shape[1] * K
+            codes = keep.tile([P, width], U32, name="codes", tag=tag, align_bytes=64)
+            scales = keep.tile([P, width], U8, name=name + "_scales", align_bytes=64)
+            nc.vector.quantize_mx(out=codes[:].bitcast(E4M3), scales=scales[:],
+                                  in_=rounded[:].rearrange("p g k j -> p (g k j)"))
             return codes, scales
 
-        def product(bank, codes, scales, first, moving, moving_scales):
+        def product(bank, codes, scales, matrix, moving, first):
             for o in range(PASSES):
-                cols = slice((first + o) * K, (first + o + 1) * K)
+                cols = slice((matrix * PASSES + o) * K, (matrix * PASSES + o + 1) * K)
                 nc.tensor.matmul_mx(out=bank[:], lhsT=codes[:, cols].bitcast(E4M3), lhsT_scale=scales[:, cols],
-                                    rhs=moving[o].bitcast(E5M2), rhs_scale=moving_scales[o],
+                                    rhs=moving[o].bitcast(E5M2), rhs_scale=planes[o][:, first:first + C],
                                     start=(o == 0), stop=(o == PASSES - 1))
 
-        def gather_bytes(h, tag):
-            packed = keep.tile([P, S // 2], U8, name="packed", tag=tag, align_bytes=64)
-            for i in range(2):
-                a = (2 * h + i) * (PAIR // 16)
-                nc.vector.tensor_copy(packed[:, i * PAIR:(i + 1) * PAIR], planes[:].indirect(slot_token[:, a:a + PAIR // 16]))
-            return packed
+        def entries(table, first, count):
+            return table[:, first // PER_COLUMN:(first + count) // PER_COLUMN]
 
-        packed = [gather_bytes(h, f"packed{h}") for h in range(2)]
-        raws = [load_w(e) for e in range(4)]
-        for o in range(PASSES):
-            load_words(o)
-        raws.extend(load_w(e) for e in range(4, 6))
-        spread(packed[0], S // 2)
+        def gather_scales(h):
+            staged = keep.tile([P, S // 2], U8, name=f"slot_scales{h}", align_bytes=64)
+            for i in range(2):
+                nc.vector.tensor_copy(staged[:, i * PAIR:(i + 1) * PAIR],
+                                      token_scales[:].indirect(entries(slot_token, (2 * h + i) * PAIR, PAIR)))
+            return staged
+
+        slot_scales = [gather_scales(h) for h in range(2)]
+        raws = [load_w(e) for e in range(E // 2)]
         nc.sync.dma_start(gate_rows[0:turned_blocks, :], gate[0, 0:TURNED * C].rearrange("(b m) -> b m", m=P))
-        raws.extend(load_w(e) for e in range(6, E + 1))
+        for o in range(PASSES):
+            nc.sync.dma_start(words[:, o * T:(o + 1) * T], dy_words[o].rearrange("p t d -> p (t d)").bitcast(I32))
+        raws.extend(load_w(e) for e in range(E // 2, E - 2))
+        fill_planes(slot_scales[0][:], 0)
+        raws.extend(load_w(e) for e in range(E - 2, E + 1))
         gate_tail = keep.tile([P, S - TURNED * C], F32, name="gate_tail")
         nc.sync.dma_start(gate_tail[:], gate[:, TURNED * C:])
-        slot_lists = []
+        token_slot = []
         for r, pos in enumerate((pos1, pos2, pos3, pos4)):
-            t = lists.tile([P, T // 16], U16, name=f"slot_list{r}")
-            nc.sync.dma_start(t[:], pos)
-            slot_lists.append(t)
+            table = lists.tile([P, T // PER_COLUMN], U16, name=f"token_slot{r}")
+            nc.sync.dma_start(table[:], pos)
+            token_slot.append(table)
+        fill_planes(slot_scales[1][:, 0:PAIR], 2 * PAIR)
 
-        windows = [words[o][:].bitcast(U32) for o in range(PASSES)]
+        windows = [words[:, o * T:(o + 1) * T + SPARE].bitcast(U32) for o in range(PASSES)]
 
         def gather_words(c, tag, piece):
-            got = keep.tile([P, PASSES * PAIR], U32, name="got", tag=tag, align_bytes=64)
+            slot_words = keep.tile([P, PASSES * PAIR], U32, name="slot_words", tag=tag, align_bytes=64)
             for a in range(0, PAIR, piece):
                 for o in range(PASSES):
-                    cols = slice((c * PAIR + a) // 16, (c * PAIR + a + piece) // 16)
-                    nc.vector.tensor_copy(got[:, o * PAIR + a:o * PAIR + a + piece], windows[o].indirect(slot_token[:, cols]))
-            return got
+                    nc.vector.tensor_copy(slot_words[:, o * PAIR + a:o * PAIR + a + piece],
+                                          windows[o].indirect(entries(slot_token, c * PAIR + a, piece)))
+            return slot_words
 
-        got = {0: gather_words(0, "got0", PAIR)}
-        roundeds = [round_w(raws[2 * c:2 * c + 2], f"stage{c}") for c in range(E // 2)]
+        pairs = E // 2
+        slot_words = gather_words(0, "first_words", PAIR)
+        roundeds = [round_w(raws[2 * c:2 * c + 2], f"stage{c}") for c in range(pairs)]
+
         gate_bank = psum.tile([P, P], F32, name="gate_bank", tag="G")
         nc.tensor.transpose(gate_bank[:], gate_rows[:], identity[:])
-        gate_cols = keep.tile([P, turned_blocks], F32, name="gate_cols", tag="raw5", align_bytes=64)
-        nc.scalar.copy(gate_cols[:], gate_bank[:, 0:turned_blocks])
-
+        gate_columns = keep.tile([P, turned_blocks], F32, name="gate_columns", tag=f"raw{E - 3}", align_bytes=64)
+        nc.scalar.copy(gate_columns[:], gate_bank[:, 0:turned_blocks])
 
         dx = keep.tile([P, S], F32, name="dx")
-        banks = {}
-        product_tag = "ACBDACGE"
-        turned_tag = "BDAC"
-        back_tag = "EFEF"
+        banks = []
 
         def turn(bank, source):
-            for b in range(C // P):
-                nc.tensor.transpose(bank[:, b * P:(b + 1) * P], source[:, b * P:(b + 1) * P], identity[:])
+            for a in range(0, source.shape[1], P):
+                nc.tensor.transpose(bank[:, a:a + P], source[:, a:a + P], identity[:])
 
-        def gate_turned(e, plain):
+        def gate_on_scalar(e, plain):
             nc.scalar.copy(plain, banks[e][:])
-            turned = psum.tile([P, C], F32, name="turned", tag=turned_tag[e])
+            turned = psum.tile([P, C], F32, name="turned", tag=TURNED_BANK[e])
             turn(turned, plain)
             gated = keep.tile([P, C], F32, name="gated", bufs=3)
-            for b in range(C // P):
-                col = e * (C // P) + b
-                nc.scalar.activation(gated[:, b * P:(b + 1) * P], turned[:, b * P:(b + 1) * P], COPY, scale=gate_cols[:, col:col + 1])
-            back = psum.tile([P, C], F32, name="back", tag=back_tag[e])
+            for b in range(BLOCKS):
+                column = e * BLOCKS + b
+                nc.scalar.activation(gated[:, b * P:(b + 1) * P], turned[:, b * P:(b + 1) * P], COPY,
+                                     scale=gate_columns[:, column:column + 1])
+            back = psum.tile([P, C], F32, name="back", tag=BACK_BANK[e])
             turn(back, gated)
             nc.scalar.copy(dx[:, e * C:(e + 1) * C], back[:])
 
-        for c in range(E // 2):
-            codes, scales = quantize_w(roundeds[c], 2, f"pair{c}", f"codes{c}")
+        for c in range(pairs):
+            codes, scales = quantize_w(roundeds[c], f"pair{c}", f"codes{c}")
             if c > 0:
-                got[c] = gather_words(c, f"stage{c}", PAIR if c < 2 else C)
+                slot_words = gather_words(c, f"stage{c}", PAIR if c < pairs - 1 else C)
+            if c == 1:
+                fill_planes(slot_scales[1][:, PAIR:], 0)
+            if c == 2:
+                fill_planes(token_scales[:, 0:T], PAIR)
             if 2 * c < TURNED:
                 plain = keep.tile([P, PAIR], F32, name="plain", tag=f"raw{E - 1 - c}", align_bytes=64)
-            if c == 2:
-                spread(packed[1], S // 2)
-            if c == 3:
-                spread(planes, T)
             for i in range(2):
                 e = 2 * c + i
-                banks[e] = psum.tile([P, C], F32, name="bank", tag=product_tag[e])
-                a = e * C % (S // 2)
-                product(banks[e], codes, scales, 2 * i,
-                        [got[c][:, o * PAIR + i * C:o * PAIR + (i + 1) * C] for o in range(PASSES)],
-                        [plane[:, a:a + C] for plane in live_planes])
+                banks.append(psum.tile([P, C], F32, name="bank", tag=PRODUCT_BANK[e]))
+                product(banks[e], codes, scales, i,
+                        [slot_words[:, o * PAIR + i * C:o * PAIR + (i + 1) * C] for o in range(PASSES)],
+                        e * C % PLANE_COLUMNS)
                 if e < TURNED:
-                    gate_turned(e, plain[:, i * C:(i + 1) * C])
+                    gate_on_scalar(e, plain[:, i * C:(i + 1) * C])
 
-        codes, scales = quantize_w(round_w(raws[E:], "raw6"), 1, "shared", "codes2")
+        codes, scales = quantize_w(round_w(raws[E:], f"raw{E - 2}"), "shared", "codes2")
         for e in range(TURNED, E):
-            nc.vector.tensor_tensor(dx[:, e * C:(e + 1) * C], banks[e][:], gate_tail[:, (e - TURNED) * C:(e - TURNED + 1) * C], MULT)
+            nc.vector.tensor_tensor(dx[:, e * C:(e + 1) * C], banks[e][:],
+                                    gate_tail[:, (e - TURNED) * C:(e - TURNED + 1) * C], MULT)
 
-        ds = [None, None]
-        for h, tag in ((1, "A"), (0, "C")):
-            cols = slice(h * C, (h + 1) * C)
+        ds = {}
+        for h, tag in ((1, PRODUCT_BANK[TURNED]), (0, PRODUCT_BANK[TURNED + 1])):
             bank = psum.tile([P, C], F32, name="shared_bank", tag=tag)
             product(bank, codes, scales, 0,
-                    [words[o][:, cols] for o in range(PASSES)],
-                    [plane[:, cols] for plane in live_planes])
+                    [words[:, o * T + h * C:o * T + (h + 1) * C] for o in range(PASSES)], PAIR + h * C)
             ds[h] = keep.tile([P, C], F32, name=f"ds{h}")
             nc.scalar.copy(ds[h][:], bank[:])
+
+        quarter = C // 2
 
         def add_on_tensor(h, count, tags):
             terms = [ds[h]]
             for r in range(count):
                 fetched = keep.tile([P, C], F32, name=f"fetched{h}_{r}")
-                nc.vector.tensor_copy(fetched[:], dx[:].indirect(slot_lists[r][:, h * (C // 16):(h + 1) * (C // 16)]))
+                nc.vector.tensor_copy(fetched[:], dx[:].indirect(entries(token_slot[r], h * C, C)))
                 terms.append(fetched)
-            width = C // len(tags)
-            turned = [psum.tile([P, width], F32, name="turned_sum", tag=pair[0]) for pair in tags]
+            sums = [psum.tile([P, quarter], F32, name="turned_sum", tag=both[0]) for both in tags]
             for n, term in enumerate(terms):
-                for b in range(C // P):
-                    i, a = divmod(b * P, width)
-                    nc.tensor.matmul(turned[i][:, a:a + P], term[:, b * P:(b + 1) * P], identity[:], is_transpose=True,
-                                     start=(n == 0 and a == 0), stop=(n == count and a + P == width))
+                for b in range(BLOCKS):
+                    i, a = divmod(b * P, quarter)
+                    nc.tensor.matmul(sums[i][:, a:a + P], term[:, b * P:(b + 1) * P], identity[:], is_transpose=True,
+                                     start=(n == 0 and a == 0), stop=(n == count and a + P == quarter))
             totals = []
-            for i, pair in enumerate(tags):
-                held = keep.tile([P, width], F32, name=f"held{h}_{i}")
-                nc.scalar.copy(held[:], turned[i][:])
-                back = psum.tile([P, width], F32, name="back_sum", tag=pair[1])
-                for a in range(0, width, P):
-                    nc.tensor.transpose(back[:, a:a + P], held[:, a:a + P], identity[:])
-                total = keep.tile([P, width], F32, name=f"total{h}_{i}")
+            for i, both in enumerate(tags):
+                held = keep.tile([P, quarter], F32, name=f"held{h}_{i}")
+                nc.scalar.copy(held[:], sums[i][:])
+                back = psum.tile([P, quarter], F32, name="back_sum", tag=both[1])
+                turn(back, held)
+                total = keep.tile([P, quarter], F32, name=f"total{h}_{i}")
                 nc.scalar.copy(total[:], back[:])
                 totals.append(total)
             return totals
 
-        partial = add_on_tensor(1, 2, ["GH"])[0]
-        for i, total in enumerate(add_on_tensor(0, 4, ["BE", "DF"])):
-            nc.scalar.dma_start(out[:, i * (C // 2):(i + 1) * (C // 2)], total[:])
-        quarter = C // 2
-        sums = [partial[:, 0:quarter], partial[:, quarter:C]]
+        upper = add_on_tensor(1, 2, ["GH", "BD"])
+        for i, total in enumerate(add_on_tensor(0, 4, ["GE", "BF"])):
+            nc.scalar.dma_start(out[:, i * quarter:(i + 1) * quarter], total[:])
         for r in (2, 3):
             for i in range(2):
                 total = keep.tile([P, quarter], F32, name=f"last{r}_{i}")
-                a = (C + i * quarter) // 16
-                nc.vector.tensor_tensor(total[:], dx[:].indirect(slot_lists[r][:, a:a + quarter // 16]), sums[i], ADD)
-                sums[i] = total[:]
+                nc.vector.tensor_tensor(total[:], dx[:].indirect(entries(token_slot[r], C + i * quarter, quarter)),
+                                        upper[i][:], ADD)
+                upper[i] = total
         for i in range(2):
-            nc.sync.dma_start(out[:, C + i * quarter:C + (i + 1) * quarter], sums[i])
+            nc.sync.dma_start(out[:, C + i * quarter:C + (i + 1) * quarter], upper[i][:])

from contextlib import ExitStack

import concourse.mybir as mybir
from concourse.masks import make_identity

F32 = mybir.dt.float32
BF16 = mybir.dt.bfloat16
I32 = mybir.dt.int32
U32 = mybir.dt.uint32
U16 = mybir.dt.uint16
U8 = mybir.dt.uint8
E4M3 = mybir.dt.float8_e4m3fn_x4
E5M2 = mybir.dt.float8_e5m2_x4
MULT = mybir.AluOpType.mult
ADD = mybir.AluOpType.add
COPY = mybir.ActivationFunctionType.Copy

P = 128
K, T, E, C, N = 128, 1024, 8, 512, 1024
S = E * C
PASSES = 2
PACK = 4
QUADRANT = 32
PER_COLUMN = 16
PAIR = 2 * C
BLOCKS = C // P
SPARE = 352
STAGED_ROW = QUADRANT - PASSES * PACK
PLANE_ROWS = 3 * QUADRANT + PACK
PLANE_COLUMNS = 3 * PAIR
TURNED = 4
FLOPS = 2 * K * N * (S + T)

PRODUCT_BANK = "ACBDACEF"
TURNED_BANK = "BDAC"
BACK_BANK = "EFEF"


def tile_moe_bds_lin_none_kernel(tc, dy_words, dy_scales, w, gate, offs, pos1, pos2, pos3, pos4, out):
    nc = tc.nc
    with ExitStack() as ctx:
        lists = ctx.enter_context(tc.tile_pool(name="lists", bufs=1))
        keep = ctx.enter_context(tc.tile_pool(name="keep", bufs=1))
        psum = ctx.enter_context(tc.psum_pool(name="psum", bufs=1))

        slot_token = lists.tile([P, S // PER_COLUMN], U16, name="slot_token")
        nc.sync.dma_start(slot_token[:], offs)

        words = keep.tile([P, PASSES * T + SPARE], I32, name="words", align_bytes=64)
        token_scales = keep.tile([P, T + SPARE], U8, name="token_scales", align_bytes=64)
        for q in range(P // QUADRANT):
            row = QUADRANT * q
            nc.sync.dma_start(token_scales[row + STAGED_ROW:row + QUADRANT, 0:T].bitcast(I32),
                              dy_scales[:, PACK * q:PACK * (q + 1), :].bitcast(I32))
            nc.vector.memset(token_scales[row:row + STAGED_ROW, 0:T].bitcast(I32), 0)
        nc.vector.memset(token_scales[:, T:].bitcast(I32), 0)
        nc.vector.memset(words[:, PASSES * T:], 0)
        identity = keep.tile([P, P], F32, name="identity")
        make_identity(nc, identity[:])
        gate_rows = keep.tile([P, P], F32, name="gate_rows")
        nc.gpsimd.memset(gate_rows[:], 0.0)
        turned_blocks = TURNED * BLOCKS

        planes = [keep.tile([P, PLANE_COLUMNS], U8, name=f"plane{o}", align_bytes=64) for o in range(PASSES)]
        for plane in planes:
            nc.vector.memset(plane[:].bitcast(I32), 0)

        def fill_planes(staged, first):
            width = staged.shape[1]
            for o in range(PASSES):
                row = STAGED_ROW + PACK * o
                nc.sync.dma_start(planes[o][0:PLANE_ROWS, first:first + width].bitcast(I32),
                                  staged[row:row + PLANE_ROWS, :].bitcast(I32))

        def load_w(e):
            raw = keep.tile([P, PASSES, PACK, K], F32, name="raw", tag=f"raw{e}", align_bytes=64)
            nc.sync.dma_start(raw[:].rearrange("p o j k -> p o (j k)"),
                              w[e].rearrange("(o p j) k -> p o (j k)", o=PASSES, j=PACK))
            return raw

        def round_w(sources, tag):
            rounded = keep.tile([P, len(sources) * PASSES, K, PACK], BF16, name="rounded", tag=tag, align_bytes=64)
            for i, raw in enumerate(sources):
                nc.scalar.copy(rounded[:, i * PASSES:(i + 1) * PASSES], raw[:].rearrange("p o j k -> p o k j"))
            return rounded

        def quantize_w(rounded, name, tag):
            width = rounded.shape[1] * K
            codes = keep.tile([P, width], U32, name="codes", tag=tag, align_bytes=64)
            scales = keep.tile([P, width], U8, name=name + "_scales", align_bytes=64)
            nc.vector.quantize_mx(out=codes[:].bitcast(E4M3), scales=scales[:],
                                  in_=rounded[:].rearrange("p g k j -> p (g k j)"))
            return codes, scales

        def product(bank, codes, scales, matrix, moving, first):
            for o in range(PASSES):
                cols = slice((matrix * PASSES + o) * K, (matrix * PASSES + o + 1) * K)
                nc.tensor.matmul_mx(out=bank[:], lhsT=codes[:, cols].bitcast(E4M3), lhsT_scale=scales[:, cols],
                                    rhs=moving[o].bitcast(E5M2), rhs_scale=planes[o][:, first:first + C],
                                    start=(o == 0), stop=(o == PASSES - 1))

        def entries(table, first, count):
            return table[:, first // PER_COLUMN:(first + count) // PER_COLUMN]

        def gather_scales(h):
            staged = keep.tile([P, S // 2], U8, name=f"slot_scales{h}", align_bytes=64)
            for i in range(2):
                nc.vector.tensor_copy(staged[:, i * PAIR:(i + 1) * PAIR],
                                      token_scales[:].indirect(entries(slot_token, (2 * h + i) * PAIR, PAIR)))
            return staged

        slot_scales = [gather_scales(h) for h in range(2)]
        raws = [load_w(e) for e in range(E // 2)]
        nc.sync.dma_start(gate_rows[0:turned_blocks, :], gate[0, 0:TURNED * C].rearrange("(b m) -> b m", m=P))
        for o in range(PASSES):
            nc.sync.dma_start(words[:, o * T:(o + 1) * T], dy_words[o].rearrange("p t d -> p (t d)").bitcast(I32))
        raws.extend(load_w(e) for e in range(E // 2, E - 2))
        fill_planes(slot_scales[0][:], 0)
        raws.extend(load_w(e) for e in range(E - 2, E + 1))
        gate_tail = keep.tile([P, S - TURNED * C], F32, name="gate_tail")
        nc.sync.dma_start(gate_tail[:], gate[:, TURNED * C:])
        token_slot = []
        for r, pos in enumerate((pos1, pos2, pos3, pos4)):
            table = lists.tile([P, T // PER_COLUMN], U16, name=f"token_slot{r}")
            nc.sync.dma_start(table[:], pos)
            token_slot.append(table)
        fill_planes(slot_scales[1][:, 0:PAIR], 2 * PAIR)

        windows = [words[:, o * T:(o + 1) * T + SPARE].bitcast(U32) for o in range(PASSES)]

        def gather_words(c, tag, piece):
            slot_words = keep.tile([P, PASSES * PAIR], U32, name="slot_words", tag=tag, align_bytes=64)
            for a in range(0, PAIR, piece):
                for o in range(PASSES):
                    nc.vector.tensor_copy(slot_words[:, o * PAIR + a:o * PAIR + a + piece],
                                          windows[o].indirect(entries(slot_token, c * PAIR + a, piece)))
            return slot_words

        pairs = E // 2
        slot_words = gather_words(0, "first_words", PAIR)
        roundeds = [round_w(raws[2 * c:2 * c + 2], f"stage{c}") for c in range(pairs)]

        gate_bank = psum.tile([P, P], F32, name="gate_bank", tag="G")
        nc.tensor.transpose(gate_bank[:], gate_rows[:], identity[:])
        gate_columns = keep.tile([P, turned_blocks], F32, name="gate_columns", tag=f"raw{E - 3}", align_bytes=64)
        nc.scalar.copy(gate_columns[:], gate_bank[:, 0:turned_blocks])

        dx = keep.tile([P, S], F32, name="dx")
        banks = []

        def turn(bank, source):
            for a in range(0, source.shape[1], P):
                nc.tensor.transpose(bank[:, a:a + P], source[:, a:a + P], identity[:])

        def gate_on_scalar(e, plain):
            nc.scalar.copy(plain, banks[e][:])
            turned = psum.tile([P, C], F32, name="turned", tag=TURNED_BANK[e])
            turn(turned, plain)
            gated = keep.tile([P, C], F32, name="gated", bufs=3)
            for b in range(BLOCKS):
                column = e * BLOCKS + b
                nc.scalar.activation(gated[:, b * P:(b + 1) * P], turned[:, b * P:(b + 1) * P], COPY,
                                     scale=gate_columns[:, column:column + 1])
            back = psum.tile([P, C], F32, name="back", tag=BACK_BANK[e])
            turn(back, gated)
            nc.scalar.copy(dx[:, e * C:(e + 1) * C], back[:])

        for c in range(pairs):
            codes, scales = quantize_w(roundeds[c], f"pair{c}", f"codes{c}")
            if c > 0:
                slot_words = gather_words(c, f"stage{c}", PAIR if c < pairs - 1 else C)
            if c == 1:
                fill_planes(slot_scales[1][:, PAIR:], 0)
            if c == 2:
                fill_planes(token_scales[:, 0:T], PAIR)
            if 2 * c < TURNED:
                plain = keep.tile([P, PAIR], F32, name="plain", tag=f"raw{E - 1 - c}", align_bytes=64)
            for i in range(2):
                e = 2 * c + i
                banks.append(psum.tile([P, C], F32, name="bank", tag=PRODUCT_BANK[e]))
                product(banks[e], codes, scales, i,
                        [slot_words[:, o * PAIR + i * C:o * PAIR + (i + 1) * C] for o in range(PASSES)],
                        e * C % PLANE_COLUMNS)
                if e < TURNED:
                    gate_on_scalar(e, plain[:, i * C:(i + 1) * C])

        codes, scales = quantize_w(round_w(raws[E:], f"raw{E - 2}"), "shared", "codes2")
        for e in range(TURNED, E):
            nc.vector.tensor_tensor(dx[:, e * C:(e + 1) * C], banks[e][:],
                                    gate_tail[:, (e - TURNED) * C:(e - TURNED + 1) * C], MULT)

        ds = {}
        for h, tag in ((1, PRODUCT_BANK[TURNED]), (0, PRODUCT_BANK[TURNED + 1])):
            bank = psum.tile([P, C], F32, name="shared_bank", tag=tag)
            product(bank, codes, scales, 0,
                    [words[:, o * T + h * C:o * T + (h + 1) * C] for o in range(PASSES)], PAIR + h * C)
            ds[h] = keep.tile([P, C], F32, name=f"ds{h}")
            nc.scalar.copy(ds[h][:], bank[:])

        quarter = C // 2

        def add_on_tensor(h, count, tags):
            terms = [ds[h]]
            for r in range(count):
                fetched = keep.tile([P, C], F32, name=f"fetched{h}_{r}")
                nc.vector.tensor_copy(fetched[:], dx[:].indirect(entries(token_slot[r], h * C, C)))
                terms.append(fetched)
            sums = [psum.tile([P, quarter], F32, name="turned_sum", tag=both[0]) for both in tags]
            for n, term in enumerate(terms):
                for b in range(BLOCKS):
                    i, a = divmod(b * P, quarter)
                    nc.tensor.matmul(sums[i][:, a:a + P], term[:, b * P:(b + 1) * P], identity[:], is_transpose=True,
                                     start=(n == 0 and a == 0), stop=(n == count and a + P == quarter))
            totals = []
            for i, both in enumerate(tags):
                held = keep.tile([P, quarter], F32, name=f"held{h}_{i}")
                nc.scalar.copy(held[:], sums[i][:])
                back = psum.tile([P, quarter], F32, name="back_sum", tag=both[1])
                turn(back, held)
                total = keep.tile([P, quarter], F32, name=f"total{h}_{i}")
                nc.scalar.copy(total[:], back[:])
                totals.append(total)
            return totals

        upper = add_on_tensor(1, 2, ["GH", "BD"])
        for i, total in enumerate(add_on_tensor(0, 4, ["GE", "BF"])):
            nc.scalar.dma_start(out[:, i * quarter:(i + 1) * quarter], total[:])
        for r in (2, 3):
            for i in range(2):
                total = keep.tile([P, quarter], F32, name=f"last{r}_{i}")
                nc.vector.tensor_tensor(total[:], dx[:].indirect(entries(token_slot[r], C + i * quarter, quarter)),
                                        upper[i][:], ADD)
                upper[i] = total
        for i in range(2):
            nc.sync.dma_start(out[:, C + i * quarter:C + (i + 1) * quarter], upper[i][:])
